import numpy as np, ml_dtypes
CORES = [4,20,60,84,92,100,116]
N = 7
import mx_ref
NC, G, MB = 128, 2, 3
C = np.float32(0.037)
BF = ml_dtypes.bfloat16
def cut(t, i, w=512):
    return t[:, w * i:w * i + w]
def tile(rs):
    return np.stack(rs, axis=2).reshape(128, -1).astype(BF)
def layer(w, X):
    out = []
    for i in range(G):
        for t in range(len(X)):
            p = mx_ref.matmul(mx_ref.quantize(cut(w, len(X) * i + t)), X[t])
            z = p if t == 0 else z + p
        out.append(z)
    return out
def act(Z):
    return [np.maximum(s * z, 0) * C for z in Z for s in (1, -1)]
def masked(U, Z):
    return [(s * u * (s * z > 0)) * C for u, z in zip(U, Z) for s in (1, -1)]
def setup_inputs(rng):
    def f(*shape):
        return mx_ref.flush((rng.standard_normal(shape, dtype=np.float32) * np.exp2(rng.integers(-2, 3, shape[:-1] + (1,)))).astype(BF))
    return {"x": f(N, 128, MB * 4 * NC), "e": f(N, 128, MB * 4 * NC), "w": f(N, 128, G * 512), "v": f(N, 128, G * 512)}
def setup_inputs_blocks(rng):
    d = setup_inputs(rng)
    for k in ("x", "e"): d[k] = mx_ref.spread(d[k], rng, 4)
    for k in ("w", "v"): d[k] = mx_ref.spread(d[k], rng, 1)
    return d
def setup_inputs_wide(rng):
    d = setup_inputs(rng)
    for k in ("x", "e"): d[k] = mx_ref.flush((d[k].astype(np.float32) * np.exp2(rng.integers(-8, 9, (N, 1, 1))).astype(np.float32)).astype(BF))
    return d
def setup_inputs_zeros(rng):
    d = setup_inputs(rng); v = d["x"].reshape(N, 128, -1, 4).copy()
    v[np.broadcast_to((rng.random((N, 1, v.shape[2], 1)) < 0.33), v.shape)] = 0
    d["x"] = v.reshape(d["x"].shape)
    return d
def reference(x, e, w, v):
    y = np.full((N, 128, MB * G * NC), np.nan, np.float32)
    for m in range(MB):
        a = mx_ref.quantize(cut(x[N - 1], m, 4 * NC)); Z = []
        for s in range(N):
            Z.append(layer(w[s], [a]))
            if s < N - 1: a = mx_ref.quantize(tile(act(Z[s])))
        b = mx_ref.quantize(cut(e[0], m, 4 * NC))
        for s in range(N - 1, 0, -1):
            b = mx_ref.quantize(tile(masked(layer(v[s], [b]), Z[s])))
        U = layer(v[0], [b])
        for i in range(G):
            y[0][:, NC * (G * m + i):NC * (G * m + i) + NC] = U[i] * (Z[0][i] > 0)
    return {"y": y}

@@ -1,0 +1,245 @@
+import numpy as np
+from concourse.mybir import dt, AluOpType, ActivationFunctionType
+
+MB, NC, G = 3, 128, 2
+C = float(np.float32(0.037))
+
+SCRATCH = {
+    "xt": ("sbuf", [128, MB * 512], "bfloat16"),
+    "et": ("sbuf", [128, MB * 512], "bfloat16"),
+    "wt": ("sbuf", [128, G * 512], "bfloat16"),
+    "vt": ("sbuf", [128, G * 512], "bfloat16"),
+    "ta": ("sbuf", [128, MB * 512], "bfloat16"),
+    "tb": ("sbuf", [128, MB * 512], "bfloat16"),
+    "fm": ("sbuf", [128, MB * 512], "float32"),
+    "yt": ("sbuf", [128, MB * G * NC], "float32"),
+    "zu": ("psum", [128, 512 * 8], "float32"),
+}
+for _k, _n in (("w", G), ("v", G), ("e", MB), ("x", MB), ("i", MB), ("o", MB), ("b", MB), ("p", MB)):
+    SCRATCH["c" + _k + "q"] = ("sbuf", [128, _n * NC], "float8_e4m3fn_x4")
+    SCRATCH["c" + _k + "s"] = ("sbuf", [128, _n * NC], "uint8")
+_PER_TILE = ["ra", "rb", "ec", "ep", "lx", "le", "qx", "qe", "qa", "qb", "z0_", "z1_", "ta", "fm", "u0_", "u1_", "tb", "y0_", "y1_"]
+SEMAPHORES = [k + str(m) for k in _PER_TILE for m in range(MB)] + ["lw", "lv", "qw", "qv", "sent", "st0", "st1"]
+PARTS = ("q", "s")
+
+
+def passers(src, dst, topo):
+    if topo.may_write(src, dst):
+        return ()
+    near = [k for k in range(128) if k != src and topo.chip(k) == topo.chip(src) and topo.may_write(k, dst)]
+    near.sort(key=lambda k: (topo.die(k) != topo.die(src), k))
+    return near[0], near[1]
+
+
+def plan(cores, topo):
+    n = len(cores)
+    msgs = []
+
+    def way(s, t, part):
+        p = passers(cores[s], cores[t], topo)
+        return [cores[s]] + ([p[part]] if p else []) + [cores[t]]
+
+    for m in range(MB):
+        for part in (0, 1):
+            k = PARTS[part]
+            msgs.append((10 + m, 10 + m, way(n - 1, 0, part), "cx" + k, "ci" + k, m, "qx", "ra"))
+            for s in range(n - 1):
+                msgs.append((20 + m, 20 + m, way(s, s + 1, part), "co" + k, "ci" + k, m, "qa", "ra"))
+                msgs.append((40 + m, 40 + m, way(s + 1, s, part), "cp" + k, "cb" + k, m, "qb", "rb"))
+    direct = [s for s in range(1, n - 1) if topo.may_write(cores[0], cores[s])]
+    behind = [s for s in range(1, n - 1) if s not in direct]
+    for part in (0, 1):
+        k, land = PARTS[part], ("ec", "ep")[part]
+        for m, s, home in ((0, behind[0], 2), (1, behind[1], 30)):
+            path = [cores[0], passers(cores[s - 1], cores[s], topo)[part], cores[s],
+                    passers(cores[s], cores[s + 1], topo)[part], cores[n - 1]]
+            msgs.append((m, home, path, "ce" + k, "ce" + k, m, "qe", land))
+        path = [cores[0]]
+        for s in direct:
+            path.append(cores[s])
+            p = passers(cores[s], cores[s + 1], topo) or passers(cores[s], cores[s - 1], topo)
+            if part or s == direct[-1]:
+                path.append(p[part])
+        msgs.append((2, 1, path + [cores[n - 1]], "ce" + k, "ce" + k, 2, "qe", land))
+    return msgs
+
+
+def rank_program(g, core, T, topo):
+    cores = list(T.cores)
+    n = len(cores)
+    rank = T.rank_of(core)
+    due = {}
+    sends = []
+    for k, (place, home, path, made, land, m, made_sem, land_sem) in enumerate(plan(cores, topo)):
+        for h in range(len(path) - 1):
+            src, dst = path[h], path[h + 1]
+            if dst == core:
+                name = land_sem + str(m)
+                due[name] = due.get(name, 0) + bin(topo.mask(src, dst)).count("1")
+            if src == core:
+                sends.append((home if rank == 0 else place, k, land if h else made, land, m, (land_sem if h else made_sem) + str(m),
+                              land_sem + str(m), dst))
+    if not sends and not due:
+        return
+    sem = T.sem
+
+    def view(name, m):
+        v = T[name][:, NC * m:NC * m + NC]
+        return v.bitcast(dt.uint8) if name[-1] == "q" else v
+
+    sends.sort()
+    count = 0
+    for _, _, src_buf, dst_buf, m, wait, land, dst in sends:
+        g.wait_ge(sem[wait], due.get(wait, 1))
+        rid, pid, _ = topo.addr(dst)
+        mask = topo.mask(core, dst)
+        g.remote_dma(out_ap=view(dst_buf, m), in_ap=view(src_buf, m), remote_sem=sem[land], local_sem=sem.sent,
+                     pid=pid, routing_id=rid, dma_engine_mask=mask)
+        count += bin(mask).count("1")
+    g.wait_ge(sem.sent, count)
+    if rank is None:
+        return
+
+    first, lastr = rank == 0, rank == n - 1
+    tile = lambda t, m: t[:, 512 * m:512 * m + 512]
+    cols = lambda t, m: t[:, NC * m:NC * m + NC]
+    res = lambda t, m, b: t[:, 512 * m + b:512 * m + 512:4]
+    bank = lambda k: T.zu[:, 512 * k:512 * k + NC]
+    zbank = (lambda m, i: bank(2 * MB + i)) if lastr else (lambda m, i: bank(2 * m + i))
+    ubank = lambda m, i: bank(2 * m + i)
+    mask_at = lambda m, k: T.fm[:, 512 * m + NC * k:512 * m + NC * k + NC]
+    A, relu = AluOpType, ActivationFunctionType.Relu
+
+    if first:
+        g.sync.dma_start(tile(T.et, 2), tile(T.e, 2)).then_inc(sem.le2, 16)
+        g.scalar.dma_start(tile(T.et, 0), tile(T.e, 0)).then_inc(sem.le0, 16)
+        g.sync.dma_start(T.wt[:], T.w[:]).then_inc(sem.lw, 16)
+        g.scalar.dma_start(tile(T.et, 1), tile(T.e, 1)).then_inc(sem.le1, 16)
+        g.sync.dma_start(T.vt[:], T.v[:]).then_inc(sem.lv, 16)
+    elif lastr:
+        for m in range(MB):
+            g.sync.dma_start(tile(T.xt, m), tile(T.x, m)).then_inc(sem["lx%d" % m], 16)
+        g.scalar.wait_ge(sem.lx0, 16)
+        g.scalar.dma_start(T.vt[:], T.v[:]).then_inc(sem.lv, 16)
+        g.scalar.dma_start(T.wt[:], T.w[:]).then_inc(sem.lw, 16)
+    else:
+        g.sync.dma_start(T.wt[:], T.w[:]).then_inc(sem.lw, 16)
+        g.scalar.dma_start(T.vt[:], T.v[:]).then_inc(sem.lv, 16)
+
+    def quant(load, done, q, s, t):
+        g.vector.wait_ge(sem[load], 16)
+        g.vector.quantize_mx(q, s, t).then_inc(sem[done], 1)
+
+    def quant_w():
+        quant("lw", "qw", T.cwq[:], T.cws[:], T.wt[:])
+
+    def quant_v():
+        quant("lv", "qv", T.cvq[:], T.cvs[:], T.vt[:])
+
+    def quant_e(m):
+        quant("le%d" % m, "qe%d" % m, cols(T.ceq, m), cols(T.ces, m), tile(T.et, m))
+
+    if first:
+        quant_e(2)
+        quant_e(0)
+        quant_w()
+        quant_e(1)
+        quant_v()
+    elif lastr:
+        for m in range(MB):
+            quant("lx%d" % m, "qx%d" % m, cols(T.cxq, m), cols(T.cxs, m), tile(T.xt, m))
+        quant_v()
+        quant_w()
+    else:
+        quant_w()
+        quant_v()
+
+    def mult(out, wq, ws, i, q, s, m, done):
+        g.tensor.matmul_mx(out, cols(wq, i), cols(ws, i), cols(q, m), cols(s, m), True, True).then_inc(sem[done], 1)
+
+    def down(m):
+        name = "ra%d" % m
+        g.tensor.wait_ge(sem[name], due[name])
+        for i in range(G):
+            mult(zbank(m, i), T.cwq, T.cws, i, T.ciq, T.cis, m, "z%d_%d" % (i, m))
+
+    def back(m, q, s):
+        for i in range(G):
+            mult(ubank(m, i), T.cvq, T.cvs, i, q, s, m, "u%d_%d" % (i, m))
+
+    if lastr:
+        g.tensor.wait_ge(sem.qv, 1)
+        for m in range(MB):
+            for k in ("ec%d" % m, "ep%d" % m):
+                g.tensor.wait_ge(sem[k], due[k])
+            back(m, T.ceq, T.ces)
+            if m == 0:
+                g.tensor.wait_ge(sem.qw, 1)
+            else:
+                g.tensor.wait_ge(sem["fm%d" % (m - 1)], 4)
+            down(m)
+    else:
+        g.tensor.wait_ge(sem.qw, 1)
+        for m in range(MB):
+            down(m)
+        g.tensor.wait_ge(sem.qv, 1)
+        for m in range(MB):
+            g.tensor.wait_ge(sem["fm%d" % m], 2 if first else 4)
+            g.tensor.wait_ge(sem["rb%d" % m], due["rb%d" % m])
+            back(m, T.cbq, T.cbs)
+
+    def masks(m, i):
+        if first:
+            g.vector.tensor_scalar(mask_at(m, 2 * i), zbank(m, i), 0.0, None, A.is_gt).then_inc(sem["fm%d" % m], 1)
+        else:
+            g.vector.tensor_scalar(mask_at(m, 2 * i), zbank(m, i), 0.0, C, A.is_gt, A.mult).then_inc(sem["fm%d" % m], 1)
+            g.vector.tensor_scalar(mask_at(m, 2 * i + 1), zbank(m, i), 0.0, -C, A.is_lt, A.mult).then_inc(sem["fm%d" % m], 1)
+
+    def tile_down(m):
+        ta = sem["ta%d" % m]
+        g.scalar.wait_ge(sem["z0_%d" % m], 1)
+        g.scalar.activation(res(T.ta, m, 0), zbank(m, 0), relu, scale=C).then_inc(ta, 1)
+        g.scalar.activation(res(T.ta, m, 1), zbank(m, 0), relu, scale=-C).then_inc(ta, 1)
+        g.vector.wait_ge(sem["z1_%d" % m], 1)
+        g.vector.tensor_scalar(res(T.ta, m, 2), zbank(m, 1), C, 0.0, A.mult, A.max).then_inc(ta, 1)
+        g.vector.tensor_scalar(res(T.ta, m, 3), zbank(m, 1), -C, 0.0, A.mult, A.max).then_inc(ta, 1)
+        g.vector.wait_ge(ta, 4)
+        g.vector.quantize_mx(cols(T.coq, m), cols(T.cos, m), tile(T.ta, m)).then_inc(sem["qa%d" % m], 1)
+
+    def tile_back(m):
+        tb = sem["tb%d" % m]
+        for i in range(G):
+            g.vector.wait_ge(sem["u%d_%d" % (i, m)], 1)
+            for k in (2 * i, 2 * i + 1):
+                g.vector.tensor_tensor(res(T.tb, m, k), ubank(m, i), mask_at(m, k), A.mult).then_inc(tb, 1)
+        g.vector.wait_ge(tb, 4)
+        g.vector.quantize_mx(cols(T.cpq, m), cols(T.cps, m), tile(T.tb, m)).then_inc(sem["qb%d" % m], 1)
+
+    if lastr:
+        for m in range(MB):
+            for i in range(G):
+                g.vector.wait_ge(sem["z%d_%d" % (i, m)], 1)
+                masks(m, i)
+            g.vector.wait_ge(sem["fm%d" % m], 4)
+            tile_back(m)
+        return
+    for m in range(MB):
+        tile_down(m)
+    for m in range(MB):
+        for i in range(G):
+            masks(m, i)
+    for m in range(MB):
+        g.vector.wait_ge(sem["fm%d" % m], 2 if first else 4)
+        if not first:
+            tile_back(m)
+            continue
+        for i in range(G):
+            g.vector.wait_ge(sem["u%d_%d" % (i, m)], 1)
+            blk = slice(NC * (G * m + i), NC * (G * m + i) + NC)
+            g.vector.tensor_tensor(T.yt[:, blk], ubank(m, i), mask_at(m, 2 * i), A.mult).then_inc(sem["y%d_%d" % (i, m)], 1)
+            q, st = (g.sync, sem.st0) if i == 0 else (g.scalar, sem.st1)
+            q.wait_ge(sem["y%d_%d" % (i, m)], 1)
+            q.dma_start(T.y[:, blk], T.yt[:, blk]).then_inc(st, 16)
+    if first:
+        g.sync.wait_ge(sem.st0, 16 * MB)
+        g.scalar.wait_ge(sem.st1, 16 * MB)

@@ -2,65 +2,85 @@ import numpy as np
 from concourse.mybir import dt, AluOpType, ActivationFunctionType
 
 MB, NC, G = 3, 128, 2
+H = MB * NC // 2
+E = 4 * H
 C = float(np.float32(0.037))
+A_, B_ = 0, 1
 
 SCRATCH = {
-    "xt": ("sbuf", [128, MB * 512], "bfloat16"),
-    "et": ("sbuf", [128, MB * 512], "bfloat16"),
+    "xt": ("sbuf", [128, 2 * E], "bfloat16"),
+    "et": ("sbuf", [128, 2 * E], "bfloat16"),
     "wt": ("sbuf", [128, G * 512], "bfloat16"),
     "vt": ("sbuf", [128, G * 512], "bfloat16"),
-    "ta": ("sbuf", [128, MB * 512], "bfloat16"),
-    "tb": ("sbuf", [128, MB * 512], "bfloat16"),
-    "fm": ("sbuf", [128, MB * 512], "float32"),
-    "yt": ("sbuf", [128, MB * G * NC], "float32"),
+    "ta": ("sbuf", [128, 2 * E], "bfloat16"),
+    "tb": ("sbuf", [128, 2 * E], "bfloat16"),
+    "fm": ("sbuf", [128, 2 * E], "float32"),
+    "yt": ("sbuf", [128, 2 * G * H], "float32"),
     "zu": ("psum", [128, 512 * 8], "float32"),
 }
-for _k, _n in (("w", G), ("v", G), ("e", MB), ("x", MB), ("i", MB), ("o", MB), ("b", MB), ("p", MB)):
-    SCRATCH["c" + _k + "q"] = ("sbuf", [128, _n * NC], "float8_e4m3fn_x4")
-    SCRATCH["c" + _k + "s"] = ("sbuf", [128, _n * NC], "uint8")
-_PER_TILE = ["ra", "rb", "ec", "ep", "lx", "le", "qx", "qe", "qa", "qb", "z0_", "z1_", "ta", "fm", "u0_", "u1_", "tb", "y0_", "y1_"]
-SEMAPHORES = [k + str(m) for k in _PER_TILE for m in range(MB)] + ["lw", "lv", "qw", "qv", "sent", "st0", "st1"]
+for _k, _n in (("w", G * NC), ("v", G * NC), ("f", G * NC), ("h", G * NC), ("e", 2 * H), ("x", 2 * H), ("i", 2 * H), ("o", 2 * H),
+               ("b", 2 * H), ("p", 2 * H)):
+    SCRATCH["c" + _k + "q"] = ("sbuf", [128, _n], "float8_e4m3fn_x4")
+    SCRATCH["c" + _k + "s"] = ("sbuf", [128, _n], "uint8")
 PARTS = ("q", "s")
+SEMAPHORES = [k + p + str(c) for k in ("la", "lb", "le") for p in PARTS for c in (0, 1)]
+SEMAPHORES += [k + p for k in ("lf", "lh") for p in PARTS]
+SEMAPHORES += [k + str(c) for k in ("dx", "qx", "qe", "qa", "qb", "ta", "tb", "fm", "z0_", "z1_", "u0_", "u1_", "y0_", "y1_")
+               for c in (0, 1)]
+SEMAPHORES += ["dw", "dv", "de", "qw", "qv", "sent", "st0", "st1"]
 
 
 def passers(src, dst, topo):
     if topo.may_write(src, dst):
-        return ()
+        return []
     near = [k for k in range(128) if k != src and topo.chip(k) == topo.chip(src) and topo.may_write(k, dst)]
-    near.sort(key=lambda k: (topo.die(k) != topo.die(src), k))
-    return near[0], near[1]
+    return sorted(near, key=lambda k: (topo.die(k) != topo.die(src), k))
+
+
+def stops(cores, topo):
+    a, b = [0], [0]
+    for s in range(1, len(cores), 2):
+        r = s if topo.may_write(cores[a[-1]], cores[s]) else s + 1
+        a.append(r)
+        b.append(2 * s + 1 - r)
+    return a, b
 
 
 def plan(cores, topo):
     n = len(cores)
     msgs = []
+    ways = stops(cores, topo)
+
+    def msg(place, path, made, mslot, land, lslot, made_sem, land_sem, part):
+        k = PARTS[part]
+        msgs.append((place, path, made + k, mslot, land + k, lslot, made_sem, land_sem % k))
 
     def way(s, t, part):
         p = passers(cores[s], cores[t], topo)
         return [cores[s]] + ([p[part]] if p else []) + [cores[t]]
 
-    for m in range(MB):
-        for part in (0, 1):
-            k = PARTS[part]
-            msgs.append((10 + m, 10 + m, way(n - 1, 0, part), "cx" + k, "ci" + k, m, "qx", "ra"))
-            for s in range(n - 1):
-                msgs.append((20 + m, 20 + m, way(s, s + 1, part), "co" + k, "ci" + k, m, "qa", "ra"))
-                msgs.append((40 + m, 40 + m, way(s + 1, s, part), "cp" + k, "cb" + k, m, "qb", "rb"))
-    direct = [s for s in range(1, n - 1) if topo.may_write(cores[0], cores[s])]
-    behind = [s for s in range(1, n - 1) if s not in direct]
     for part in (0, 1):
-        k, land = PARTS[part], ("ec", "ep")[part]
-        for m, s, home in ((0, behind[0], 2), (1, behind[1], 30)):
-            path = [cores[0], passers(cores[s - 1], cores[s], topo)[part], cores[s],
-                    passers(cores[s], cores[s + 1], topo)[part], cores[n - 1]]
-            msgs.append((m, home, path, "ce" + k, "ce" + k, m, "qe", land))
-        path = [cores[0]]
-        for s in direct:
-            path.append(cores[s])
-            p = passers(cores[s], cores[s + 1], topo) or passers(cores[s], cores[s - 1], topo)
-            if part or s == direct[-1]:
-                path.append(p[part])
-        msgs.append((2, 1, path + [cores[n - 1]], "ce" + k, "ce" + k, 2, "qe", land))
+        for c in (A_, B_):
+            w = ways[c]
+            last = w[-1]
+            msg(1 - c, way(n - 1, 0, part), "cx", c, "ci", c, "qx%d" % c, "la%%s%d" % c, part)
+            p = passers(cores[0], cores[w[1]], topo)
+            path = [cores[0]] + ([p[part]] if p else []) + [cores[last]]
+            msg(5 - c, path, "ce", c, "ce", c, "qe%d" % c, "le%%s%d" % c, part)
+            for k in range(len(w) - 1):
+                msg(21 - c, way(w[k], w[k + 1], part), "co", 1 if k else c, "ci", c, "qa%d" % (1 if k else c), "la%%s%d" % c, part)
+                msg(41 - c, way(w[k + 1], w[k], part), "cp", 0, "cb", c, "qb0", "lb%%s%d" % c, part)
+            for k in range(1, len(w)):
+                s = w[k]
+                t = ways[1 - c][k]
+                p = passers(cores[s], cores[t], topo)
+                if p:
+                    pw, pv = [p[part]], [p[2 + part]]
+                else:
+                    near = passers(cores[s], cores[w[k - 1]], topo)
+                    pw, pv = ([near[part]] if near else []), []
+                msg(12, [cores[s]] + pw + [cores[t]], "cw", None, "cf", None, "qw", "lf%s", part)
+                msg(14, [cores[s]] + pv + [cores[t]], "cv", None, "ch", None, "qv", "lh%s", part)
     return msgs
 
 
@@ -70,176 +90,202 @@ def rank_program(g, core, T, topo):
     rank = T.rank_of(core)
     due = {}
     sends = []
-    for k, (place, home, path, made, land, m, made_sem, land_sem) in enumerate(plan(cores, topo)):
+    for path_no, (place, path, made, mslot, land, lslot, made_sem, land_sem) in enumerate(plan(cores, topo)):
         for h in range(len(path) - 1):
             src, dst = path[h], path[h + 1]
             if dst == core:
-                name = land_sem + str(m)
-                due[name] = due.get(name, 0) + bin(topo.mask(src, dst)).count("1")
+                due[land_sem] = due.get(land_sem, 0) + bin(topo.mask(src, dst)).count("1")
             if src == core:
-                sends.append((home if rank == 0 else place, k, land if h else made, land, m, (land_sem if h else made_sem) + str(m),
-                              land_sem + str(m), dst))
+                sends.append((place, path_no, land if h else made, lslot if h else mslot, land, lslot,
+                              land_sem if h else made_sem, land_sem, dst))
     if not sends and not due:
         return
     sem = T.sem
 
-    def view(name, m):
-        v = T[name][:, NC * m:NC * m + NC]
+    def view(name, slot):
+        v = T[name][:] if slot is None else T[name][:, H * slot:H * slot + H]
         return v.bitcast(dt.uint8) if name[-1] == "q" else v
 
-    sends.sort()
+    sends.sort(key=lambda s: s[:2])
     count = 0
-    for _, _, src_buf, dst_buf, m, wait, land, dst in sends:
+    for _, _, src_buf, src_slot, dst_buf, dst_slot, wait, land, dst in sends:
         g.wait_ge(sem[wait], due.get(wait, 1))
         rid, pid, _ = topo.addr(dst)
         mask = topo.mask(core, dst)
-        g.remote_dma(out_ap=view(dst_buf, m), in_ap=view(src_buf, m), remote_sem=sem[land], local_sem=sem.sent,
+        g.remote_dma(out_ap=view(dst_buf, dst_slot), in_ap=view(src_buf, src_slot), remote_sem=sem[land], local_sem=sem.sent,
                      pid=pid, routing_id=rid, dma_engine_mask=mask)
         count += bin(mask).count("1")
     g.wait_ge(sem.sent, count)
     if rank is None:
         return
 
+    ways = stops(cores, topo)
     first, lastr = rank == 0, rank == n - 1
-    tile = lambda t, m: t[:, 512 * m:512 * m + 512]
-    cols = lambda t, m: t[:, NC * m:NC * m + NC]
-    res = lambda t, m, b: t[:, 512 * m + b:512 * m + 512:4]
-    bank = lambda k: T.zu[:, 512 * k:512 * k + NC]
-    zbank = (lambda m, i: bank(2 * MB + i)) if lastr else (lambda m, i: bank(2 * m + i))
-    ubank = lambda m, i: bank(2 * m + i)
-    mask_at = lambda m, k: T.fm[:, 512 * m + NC * k:512 * m + NC * k + NC]
+    half = A_ if rank in ways[A_] else B_
+    turn = rank in (ways[A_][-1], ways[B_][-1])
+    tile = lambda t, c: t[:, E * c:E * c + E]
+    cols = lambda t, c: t[:, H * c:H * c + H]
+    res = lambda t, c, b: t[:, E * c + b:E * c + E:4]
+    bank = lambda k: T.zu[:, 512 * k:512 * k + H]
+    zbank = lambda c, i: bank(2 * c + i)
+    ubank = lambda c, i: bank(4 + 2 * c + i)
+    mask_at = lambda c, k: T.fm[:, E * c + H * k:E * c + H * k + H]
     A, relu = AluOpType, ActivationFunctionType.Relu
 
     if first:
-        g.sync.dma_start(tile(T.et, 2), tile(T.e, 2)).then_inc(sem.le2, 16)
-        g.scalar.dma_start(tile(T.et, 0), tile(T.e, 0)).then_inc(sem.le0, 16)
-        g.sync.dma_start(T.wt[:], T.w[:]).then_inc(sem.lw, 16)
-        g.scalar.dma_start(tile(T.et, 1), tile(T.e, 1)).then_inc(sem.le1, 16)
-        g.sync.dma_start(T.vt[:], T.v[:]).then_inc(sem.lv, 16)
+        g.sync.dma_start(T.wt[:], T.w[:]).then_inc(sem.dw, 16)
+        g.scalar.dma_start(T.et[:], T.e[:]).then_inc(sem.de, 16)
+        g.sync.dma_start(T.vt[:], T.v[:]).then_inc(sem.dv, 16)
     elif lastr:
-        for m in range(MB):
-            g.sync.dma_start(tile(T.xt, m), tile(T.x, m)).then_inc(sem["lx%d" % m], 16)
-        g.scalar.wait_ge(sem.lx0, 16)
-        g.scalar.dma_start(T.vt[:], T.v[:]).then_inc(sem.lv, 16)
-        g.scalar.dma_start(T.wt[:], T.w[:]).then_inc(sem.lw, 16)
+        g.sync.dma_start(tile(T.xt, B_), tile(T.x, B_)).then_inc(sem["dx%d" % B_], 16)
+        g.sync.dma_start(tile(T.xt, A_), tile(T.x, A_)).then_inc(sem["dx%d" % A_], 16)
+        g.scalar.wait_ge(sem["dx%d" % B_], 16)
+        g.scalar.dma_start(T.wt[:], T.w[:]).then_inc(sem.dw, 16)
+        g.scalar.dma_start(T.vt[:], T.v[:]).then_inc(sem.dv, 16)
     else:
-        g.sync.dma_start(T.wt[:], T.w[:]).then_inc(sem.lw, 16)
-        g.scalar.dma_start(T.vt[:], T.v[:]).then_inc(sem.lv, 16)
+        g.sync.dma_start(T.wt[:], T.w[:]).then_inc(sem.dw, 16)
+        g.scalar.wait_ge(sem.dw, 16)
+        g.scalar.dma_start(T.vt[:], T.v[:]).then_inc(sem.dv, 16)
 
     def quant(load, done, q, s, t):
         g.vector.wait_ge(sem[load], 16)
         g.vector.quantize_mx(q, s, t).then_inc(sem[done], 1)
 
-    def quant_w():
-        quant("lw", "qw", T.cwq[:], T.cws[:], T.wt[:])
-
-    def quant_v():
-        quant("lv", "qv", T.cvq[:], T.cvs[:], T.vt[:])
-
-    def quant_e(m):
-        quant("le%d" % m, "qe%d" % m, cols(T.ceq, m), cols(T.ces, m), tile(T.et, m))
-
-    if first:
-        quant_e(2)
-        quant_e(0)
-        quant_w()
-        quant_e(1)
-        quant_v()
-    elif lastr:
-        for m in range(MB):
-            quant("lx%d" % m, "qx%d" % m, cols(T.cxq, m), cols(T.cxs, m), tile(T.xt, m))
-        quant_v()
-        quant_w()
-    else:
-        quant_w()
-        quant_v()
-
-    def mult(out, wq, ws, i, q, s, m, done):
-        g.tensor.matmul_mx(out, cols(wq, i), cols(ws, i), cols(q, m), cols(s, m), True, True).then_inc(sem[done], 1)
-
-    def down(m):
-        name = "ra%d" % m
-        g.tensor.wait_ge(sem[name], due[name])
-        for i in range(G):
-            mult(zbank(m, i), T.cwq, T.cws, i, T.ciq, T.cis, m, "z%d_%d" % (i, m))
-
-    def back(m, q, s):
-        for i in range(G):
-            mult(ubank(m, i), T.cvq, T.cvs, i, q, s, m, "u%d_%d" % (i, m))
-
     if lastr:
-        g.tensor.wait_ge(sem.qv, 1)
-        for m in range(MB):
-            for k in ("ec%d" % m, "ep%d" % m):
-                g.tensor.wait_ge(sem[k], due[k])
-            back(m, T.ceq, T.ces)
-            if m == 0:
-                g.tensor.wait_ge(sem.qw, 1)
-            else:
-                g.tensor.wait_ge(sem["fm%d" % (m - 1)], 4)
-            down(m)
-    else:
-        g.tensor.wait_ge(sem.qw, 1)
-        for m in range(MB):
-            down(m)
-        g.tensor.wait_ge(sem.qv, 1)
-        for m in range(MB):
-            g.tensor.wait_ge(sem["fm%d" % m], 2 if first else 4)
-            g.tensor.wait_ge(sem["rb%d" % m], due["rb%d" % m])
-            back(m, T.cbq, T.cbs)
+        for c in (B_, A_):
+            quant("dx%d" % c, "qx%d" % c, cols(T.cxq, c), cols(T.cxs, c), tile(T.xt, c))
+    quant("dw", "qw", T.cwq[:], T.cws[:], T.wt[:])
+    if first:
+        for c in (B_, A_):
+            quant("de", "qe%d" % c, cols(T.ceq, c), cols(T.ces, c), tile(T.et, c))
+    quant("dv", "qv", T.cvq[:], T.cvs[:], T.vt[:])
 
-    def masks(m, i):
-        if first:
-            g.vector.tensor_scalar(mask_at(m, 2 * i), zbank(m, i), 0.0, None, A.is_gt).then_inc(sem["fm%d" % m], 1)
+    def own(layer):
+        return first or (rank - 1) % 2 == layer
+
+    def landed(name):
+        for k in PARTS:
+            nm = name % k
+            g.tensor.wait_ge(sem[nm], due[nm])
+
+    def weights(name, layer):
+        if own(layer):
+            g.tensor.wait_ge(sem["q" + name], 1)
         else:
-            g.vector.tensor_scalar(mask_at(m, 2 * i), zbank(m, i), 0.0, C, A.is_gt, A.mult).then_inc(sem["fm%d" % m], 1)
-            g.vector.tensor_scalar(mask_at(m, 2 * i + 1), zbank(m, i), 0.0, -C, A.is_lt, A.mult).then_inc(sem["fm%d" % m], 1)
+            landed("lf%s" if name == "w" else "lh%s")
 
-    def tile_down(m):
-        ta = sem["ta%d" % m]
-        g.scalar.wait_ge(sem["z0_%d" % m], 1)
-        g.scalar.activation(res(T.ta, m, 0), zbank(m, 0), relu, scale=C).then_inc(ta, 1)
-        g.scalar.activation(res(T.ta, m, 1), zbank(m, 0), relu, scale=-C).then_inc(ta, 1)
-        g.vector.wait_ge(sem["z1_%d" % m], 1)
-        g.vector.tensor_scalar(res(T.ta, m, 2), zbank(m, 1), C, 0.0, A.mult, A.max).then_inc(ta, 1)
-        g.vector.tensor_scalar(res(T.ta, m, 3), zbank(m, 1), -C, 0.0, A.mult, A.max).then_inc(ta, 1)
-        g.vector.wait_ge(ta, 4)
-        g.vector.quantize_mx(cols(T.coq, m), cols(T.cos, m), tile(T.ta, m)).then_inc(sem["qa%d" % m], 1)
+    def mult(out, wq, ws, i, q, s, slot, done):
+        g.tensor.matmul_mx(out, wq[:, NC * i:NC * i + NC], ws[:, NC * i:NC * i + NC], cols(q, slot), cols(s, slot),
+                           True, True).then_inc(sem[done], 1)
 
-    def tile_back(m):
-        tb = sem["tb%d" % m]
+    def down(c, layer, q, s, slot):
+        wq, ws = (T.cwq, T.cws) if own(layer) else (T.cfq, T.cfs)
         for i in range(G):
-            g.vector.wait_ge(sem["u%d_%d" % (i, m)], 1)
-            for k in (2 * i, 2 * i + 1):
-                g.vector.tensor_tensor(res(T.tb, m, k), ubank(m, i), mask_at(m, k), A.mult).then_inc(tb, 1)
-        g.vector.wait_ge(tb, 4)
-        g.vector.quantize_mx(cols(T.cpq, m), cols(T.cps, m), tile(T.tb, m)).then_inc(sem["qb%d" % m], 1)
+            mult(zbank(c, i), wq, ws, i, q, s, slot, "z%d_%d" % (i, c))
 
-    if lastr:
-        for m in range(MB):
-            for i in range(G):
-                g.vector.wait_ge(sem["z%d_%d" % (i, m)], 1)
-                masks(m, i)
-            g.vector.wait_ge(sem["fm%d" % m], 4)
-            tile_back(m)
-        return
-    for m in range(MB):
-        tile_down(m)
-    for m in range(MB):
+    def back(c, layer, q, s, slot):
+        vq, vs = (T.cvq, T.cvs) if own(layer) else (T.chq, T.chs)
         for i in range(G):
-            masks(m, i)
-    for m in range(MB):
-        g.vector.wait_ge(sem["fm%d" % m], 2 if first else 4)
-        if not first:
-            tile_back(m)
-            continue
-        for i in range(G):
-            g.vector.wait_ge(sem["u%d_%d" % (i, m)], 1)
-            blk = slice(NC * (G * m + i), NC * (G * m + i) + NC)
-            g.vector.tensor_tensor(T.yt[:, blk], ubank(m, i), mask_at(m, 2 * i), A.mult).then_inc(sem["y%d_%d" % (i, m)], 1)
-            q, st = (g.sync, sem.st0) if i == 0 else (g.scalar, sem.st1)
-            q.wait_ge(sem["y%d_%d" % (i, m)], 1)
-            q.dma_start(T.y[:, blk], T.yt[:, blk]).then_inc(st, 16)
+            mult(ubank(c, i), vq, vs, i, q, s, slot, "u%d_%d" % (i, c))
+
     if first:
-        g.sync.wait_ge(sem.st0, 16 * MB)
-        g.scalar.wait_ge(sem.st1, 16 * MB)
+        weights("w", 0)
+        for c in (B_, A_):
+            landed("la%%s%d" % c)
+            down(c, 0, T.ciq, T.cis, c)
+        weights("v", 0)
+        for c in (A_, B_):
+            landed("lb%%s%d" % c)
+            back(c, 0, T.cbq, T.cbs, c)
+    else:
+        weights("w", 0)
+        landed("la%%s%d" % half)
+        down(0, 0, T.ciq, T.cis, half)
+        if turn:
+            weights("v", 1)
+            landed("le%%s%d" % half)
+            back(1, 1, T.ceq, T.ces, half)
+        weights("w", 1)
+        g.tensor.wait_ge(sem.qa0, 1)
+        down(1, 1, T.coq, T.cos, 0)
+        if not turn:
+            weights("v", 1)
+            landed("lb%%s%d" % half)
+            back(1, 1, T.cbq, T.cbs, half)
+        weights("v", 0)
+        g.tensor.wait_ge(sem.qb1, 1)
+        back(0, 0, T.cpq, T.cps, 1)
+
+    def masks(c, i):
+        fm = sem["fm%d" % c]
+        if first:
+            g.vector.tensor_scalar(mask_at(c, 2 * i), zbank(c, i), 0.0, None, A.is_gt).then_inc(fm, 1)
+        else:
+            g.vector.tensor_scalar(mask_at(c, 2 * i), zbank(c, i), 0.0, C, A.is_gt, A.mult).then_inc(fm, 1)
+            g.vector.tensor_scalar(mask_at(c, 2 * i + 1), zbank(c, i), 0.0, -C, A.is_lt, A.mult).then_inc(fm, 1)
+
+    def tile_down(c):
+        ta = sem["ta%d" % c]
+        g.scalar.wait_ge(sem["z0_%d" % c], 1)
+        g.scalar.activation(res(T.ta, c, 0), zbank(c, 0), relu, scale=C).then_inc(ta, 1)
+        g.scalar.activation(res(T.ta, c, 1), zbank(c, 0), relu, scale=-C).then_inc(ta, 1)
+        g.vector.wait_ge(sem["z1_%d" % c], 1)
+        g.vector.tensor_scalar(res(T.ta, c, 2), zbank(c, 1), C, 0.0, A.mult, A.max).then_inc(ta, 1)
+        g.vector.tensor_scalar(res(T.ta, c, 3), zbank(c, 1), -C, 0.0, A.mult, A.max).then_inc(ta, 1)
+        g.vector.wait_ge(ta, 4)
+        g.vector.quantize_mx(cols(T.coq, c), cols(T.cos, c), tile(T.ta, c)).then_inc(sem["qa%d" % c], 1)
+
+    def tile_back(c):
+        tb = sem["tb%d" % c]
+        g.vector.wait_ge(sem["fm%d" % c], 4)
+        for i in range(G):
+            g.vector.wait_ge(sem["u%d_%d" % (i, c)], 1)
+            for k in (2 * i, 2 * i + 1):
+                g.vector.tensor_tensor(res(T.tb, c, k), ubank(c, i), mask_at(c, k), A.mult).then_inc(tb, 1)
+        g.vector.wait_ge(tb, 4)
+        g.vector.quantize_mx(cols(T.cpq, c), cols(T.cps, c), tile(T.tb, c)).then_inc(sem["qb%d" % c], 1)
+
+    if first:
+        for c in (B_, A_):
+            tile_down(c)
+        for c in (A_, B_):
+            for i in range(G):
+                masks(c, i)
+        stored = [0, 0]
+        for c in (A_, B_):
+            g.vector.wait_ge(sem["fm%d" % c], 2)
+            for i in range(G):
+                at = H * (G * c + i)
+                g.vector.wait_ge(sem["u%d_%d" % (i, c)], 1)
+                g.vector.tensor_tensor(T.yt[:, at:at + H], ubank(c, i), mask_at(c, 2 * i), A.mult).then_inc(sem["y%d_%d" % (i, c)], 1)
+                pieces = []
+                for m in range(MB):
+                    lo, hi = max(H * c, NC * m), min(H * c + H, NC * m + NC)
+                    if lo < hi:
+                        pieces.append((lo - hi, at + lo - H * c, NC * (G * m + i) + lo - NC * m, hi - lo))
+                pieces.sort()
+                for j, (_, fr, to, w) in enumerate(pieces):
+                    k = (i + j) % 2
+                    q, st = (g.sync, g.scalar)[k], (sem.st0, sem.st1)[k]
+                    q.wait_ge(sem["y%d_%d" % (i, c)], 1)
+                    q.dma_start(T.y[:, to:to + w], T.yt[:, fr:fr + w]).then_inc(st, 16)
+                    stored[k] += 16
+        g.sync.wait_ge(sem.st0, stored[0])
+        g.scalar.wait_ge(sem.st1, stored[1])
+        return
+    tile_down(0)
+    if turn:
+        masks(0, 0)
+        for i in range(G):
+            g.vector.wait_ge(sem["z%d_1" % i], 1)
+            masks(1, i)
+        tile_back(1)
+        masks(0, 1)
+        tile_back(0)
+    else:
+        tile_down(1)
+        for c in (1, 0):
+            for i in range(G):
+                masks(c, i)
+        tile_back(1)
+        tile_back(0)

import numpy as np
from concourse.mybir import dt, AluOpType, ActivationFunctionType

MB, NC, G = 3, 128, 2
H = MB * NC // 2
E = 4 * H
C = float(np.float32(0.037))
A_, B_ = 0, 1

SCRATCH = {
    "xt": ("sbuf", [128, 2 * E], "bfloat16"),
    "et": ("sbuf", [128, 2 * E], "bfloat16"),
    "wt": ("sbuf", [128, G * 512], "bfloat16"),
    "vt": ("sbuf", [128, G * 512], "bfloat16"),
    "ta": ("sbuf", [128, 2 * E], "bfloat16"),
    "tb": ("sbuf", [128, 2 * E], "bfloat16"),
    "fm": ("sbuf", [128, 2 * E], "float32"),
    "yt": ("sbuf", [128, 2 * G * H], "float32"),
    "zu": ("psum", [128, 512 * 8], "float32"),
}
for _k, _n in (("w", G * NC), ("v", G * NC), ("f", G * NC), ("h", G * NC), ("e", 2 * H), ("x", 2 * H), ("i", 2 * H), ("o", 2 * H),
               ("b", 2 * H), ("p", 2 * H)):
    SCRATCH["c" + _k + "q"] = ("sbuf", [128, _n], "float8_e4m3fn_x4")
    SCRATCH["c" + _k + "s"] = ("sbuf", [128, _n], "uint8")
PARTS = ("q", "s")
SEMAPHORES = [k + p + str(c) for k in ("la", "lb", "le") for p in PARTS for c in (0, 1)]
SEMAPHORES += [k + p for k in ("lf", "lh") for p in PARTS]
SEMAPHORES += [k + str(c) for k in ("dx", "qx", "qe", "qa", "qb", "ta", "tb", "fm", "z0_", "z1_", "u0_", "u1_", "y0_", "y1_")
               for c in (0, 1)]
SEMAPHORES += ["dw", "dv", "de", "qw", "qv", "sent", "st0", "st1"]


def passers(src, dst, topo):
    if topo.may_write(src, dst):
        return []
    near = [k for k in range(128) if k != src and topo.chip(k) == topo.chip(src) and topo.may_write(k, dst)]
    return sorted(near, key=lambda k: (topo.die(k) != topo.die(src), k))


def stops(cores, topo):
    a, b = [0], [0]
    for s in range(1, len(cores), 2):
        r = s if topo.may_write(cores[a[-1]], cores[s]) else s + 1
        a.append(r)
        b.append(2 * s + 1 - r)
    return a, b


def plan(cores, topo):
    n = len(cores)
    msgs = []
    ways = stops(cores, topo)

    def msg(place, path, made, mslot, land, lslot, made_sem, land_sem, part):
        k = PARTS[part]
        msgs.append((place, path, made + k, mslot, land + k, lslot, made_sem, land_sem % k))

    def way(s, t, part):
        p = passers(cores[s], cores[t], topo)
        return [cores[s]] + ([p[part]] if p else []) + [cores[t]]

    for part in (0, 1):
        for c in (A_, B_):
            w = ways[c]
            last = w[-1]
            msg(1 - c, way(n - 1, 0, part), "cx", c, "ci", c, "qx%d" % c, "la%%s%d" % c, part)
            p = passers(cores[0], cores[w[1]], topo)
            path = [cores[0]] + ([p[part]] if p else []) + [cores[last]]
            msg(5 - c, path, "ce", c, "ce", c, "qe%d" % c, "le%%s%d" % c, part)
            for k in range(len(w) - 1):
                msg(21 - c, way(w[k], w[k + 1], part), "co", 1 if k else c, "ci", c, "qa%d" % (1 if k else c), "la%%s%d" % c, part)
                msg(41 - c, way(w[k + 1], w[k], part), "cp", 0, "cb", c, "qb0", "lb%%s%d" % c, part)
            for k in range(1, len(w)):
                s = w[k]
                t = ways[1 - c][k]
                p = passers(cores[s], cores[t], topo)
                if p:
                    pw, pv = [p[part]], [p[2 + part]]
                else:
                    near = passers(cores[s], cores[w[k - 1]], topo)
                    pw, pv = ([near[part]] if near else []), []
                msg(12, [cores[s]] + pw + [cores[t]], "cw", None, "cf", None, "qw", "lf%s", part)
                msg(14, [cores[s]] + pv + [cores[t]], "cv", None, "ch", None, "qv", "lh%s", part)
    return msgs


def rank_program(g, core, T, topo):
    cores = list(T.cores)
    n = len(cores)
    rank = T.rank_of(core)
    due = {}
    sends = []
    for path_no, (place, path, made, mslot, land, lslot, made_sem, land_sem) in enumerate(plan(cores, topo)):
        for h in range(len(path) - 1):
            src, dst = path[h], path[h + 1]
            if dst == core:
                due[land_sem] = due.get(land_sem, 0) + bin(topo.mask(src, dst)).count("1")
            if src == core:
                sends.append((place, path_no, land if h else made, lslot if h else mslot, land, lslot,
                              land_sem if h else made_sem, land_sem, dst))
    if not sends and not due:
        return
    sem = T.sem

    def view(name, slot):
        v = T[name][:] if slot is None else T[name][:, H * slot:H * slot + H]
        return v.bitcast(dt.uint8) if name[-1] == "q" else v

    sends.sort(key=lambda s: s[:2])
    count = 0
    for _, _, src_buf, src_slot, dst_buf, dst_slot, wait, land, dst in sends:
        g.wait_ge(sem[wait], due.get(wait, 1))
        rid, pid, _ = topo.addr(dst)
        mask = topo.mask(core, dst)
        g.remote_dma(out_ap=view(dst_buf, dst_slot), in_ap=view(src_buf, src_slot), remote_sem=sem[land], local_sem=sem.sent,
                     pid=pid, routing_id=rid, dma_engine_mask=mask)
        count += bin(mask).count("1")
    g.wait_ge(sem.sent, count)
    if rank is None:
        return

    ways = stops(cores, topo)
    first, lastr = rank == 0, rank == n - 1
    half = A_ if rank in ways[A_] else B_
    turn = rank in (ways[A_][-1], ways[B_][-1])
    tile = lambda t, c: t[:, E * c:E * c + E]
    cols = lambda t, c: t[:, H * c:H * c + H]
    res = lambda t, c, b: t[:, E * c + b:E * c + E:4]
    bank = lambda k: T.zu[:, 512 * k:512 * k + H]
    zbank = lambda c, i: bank(2 * c + i)
    ubank = lambda c, i: bank(4 + 2 * c + i)
    mask_at = lambda c, k: T.fm[:, E * c + H * k:E * c + H * k + H]
    A, relu = AluOpType, ActivationFunctionType.Relu

    if first:
        g.sync.dma_start(T.wt[:], T.w[:]).then_inc(sem.dw, 16)
        g.scalar.dma_start(T.et[:], T.e[:]).then_inc(sem.de, 16)
        g.sync.dma_start(T.vt[:], T.v[:]).then_inc(sem.dv, 16)
    elif lastr:
        g.sync.dma_start(tile(T.xt, B_), tile(T.x, B_)).then_inc(sem["dx%d" % B_], 16)
        g.sync.dma_start(tile(T.xt, A_), tile(T.x, A_)).then_inc(sem["dx%d" % A_], 16)
        g.scalar.wait_ge(sem["dx%d" % B_], 16)
        g.scalar.dma_start(T.wt[:], T.w[:]).then_inc(sem.dw, 16)
        g.scalar.dma_start(T.vt[:], T.v[:]).then_inc(sem.dv, 16)
    else:
        g.sync.dma_start(T.wt[:], T.w[:]).then_inc(sem.dw, 16)
        g.scalar.wait_ge(sem.dw, 16)
        g.scalar.dma_start(T.vt[:], T.v[:]).then_inc(sem.dv, 16)

    def quant(load, done, q, s, t):
        g.vector.wait_ge(sem[load], 16)
        g.vector.quantize_mx(q, s, t).then_inc(sem[done], 1)

    if lastr:
        for c in (B_, A_):
            quant("dx%d" % c, "qx%d" % c, cols(T.cxq, c), cols(T.cxs, c), tile(T.xt, c))
    quant("dw", "qw", T.cwq[:], T.cws[:], T.wt[:])
    if first:
        for c in (B_, A_):
            quant("de", "qe%d" % c, cols(T.ceq, c), cols(T.ces, c), tile(T.et, c))
    quant("dv", "qv", T.cvq[:], T.cvs[:], T.vt[:])

    def own(layer):
        return first or (rank - 1) % 2 == layer

    def landed(name):
        for k in PARTS:
            nm = name % k
            g.tensor.wait_ge(sem[nm], due[nm])

    def weights(name, layer):
        if own(layer):
            g.tensor.wait_ge(sem["q" + name], 1)
        else:
            landed("lf%s" if name == "w" else "lh%s")

    def mult(out, wq, ws, i, q, s, slot, done):
        g.tensor.matmul_mx(out, wq[:, NC * i:NC * i + NC], ws[:, NC * i:NC * i + NC], cols(q, slot), cols(s, slot),
                           True, True).then_inc(sem[done], 1)

    def down(c, layer, q, s, slot):
        wq, ws = (T.cwq, T.cws) if own(layer) else (T.cfq, T.cfs)
        for i in range(G):
            mult(zbank(c, i), wq, ws, i, q, s, slot, "z%d_%d" % (i, c))

    def back(c, layer, q, s, slot):
        vq, vs = (T.cvq, T.cvs) if own(layer) else (T.chq, T.chs)
        for i in range(G):
            mult(ubank(c, i), vq, vs, i, q, s, slot, "u%d_%d" % (i, c))

    if first:
        weights("w", 0)
        for c in (B_, A_):
            landed("la%%s%d" % c)
            down(c, 0, T.ciq, T.cis, c)
        weights("v", 0)
        for c in (A_, B_):
            landed("lb%%s%d" % c)
            back(c, 0, T.cbq, T.cbs, c)
    else:
        weights("w", 0)
        landed("la%%s%d" % half)
        down(0, 0, T.ciq, T.cis, half)
        if turn:
            weights("v", 1)
            landed("le%%s%d" % half)
            back(1, 1, T.ceq, T.ces, half)
        weights("w", 1)
        g.tensor.wait_ge(sem.qa0, 1)
        down(1, 1, T.coq, T.cos, 0)
        if not turn:
            weights("v", 1)
            landed("lb%%s%d" % half)
            back(1, 1, T.cbq, T.cbs, half)
        weights("v", 0)
        g.tensor.wait_ge(sem.qb1, 1)
        back(0, 0, T.cpq, T.cps, 1)

    def masks(c, i):
        fm = sem["fm%d" % c]
        if first:
            g.vector.tensor_scalar(mask_at(c, 2 * i), zbank(c, i), 0.0, None, A.is_gt).then_inc(fm, 1)
        else:
            g.vector.tensor_scalar(mask_at(c, 2 * i), zbank(c, i), 0.0, C, A.is_gt, A.mult).then_inc(fm, 1)
            g.vector.tensor_scalar(mask_at(c, 2 * i + 1), zbank(c, i), 0.0, -C, A.is_lt, A.mult).then_inc(fm, 1)

    def tile_down(c):
        ta = sem["ta%d" % c]
        g.scalar.wait_ge(sem["z0_%d" % c], 1)
        g.scalar.activation(res(T.ta, c, 0), zbank(c, 0), relu, scale=C).then_inc(ta, 1)
        g.scalar.activation(res(T.ta, c, 1), zbank(c, 0), relu, scale=-C).then_inc(ta, 1)
        g.vector.wait_ge(sem["z1_%d" % c], 1)
        g.vector.tensor_scalar(res(T.ta, c, 2), zbank(c, 1), C, 0.0, A.mult, A.max).then_inc(ta, 1)
        g.vector.tensor_scalar(res(T.ta, c, 3), zbank(c, 1), -C, 0.0, A.mult, A.max).then_inc(ta, 1)
        g.vector.wait_ge(ta, 4)
        g.vector.quantize_mx(cols(T.coq, c), cols(T.cos, c), tile(T.ta, c)).then_inc(sem["qa%d" % c], 1)

    def tile_back(c):
        tb = sem["tb%d" % c]
        g.vector.wait_ge(sem["fm%d" % c], 4)
        for i in range(G):
            g.vector.wait_ge(sem["u%d_%d" % (i, c)], 1)
            for k in (2 * i, 2 * i + 1):
                g.vector.tensor_tensor(res(T.tb, c, k), ubank(c, i), mask_at(c, k), A.mult).then_inc(tb, 1)
        g.vector.wait_ge(tb, 4)
        g.vector.quantize_mx(cols(T.cpq, c), cols(T.cps, c), tile(T.tb, c)).then_inc(sem["qb%d" % c], 1)

    if first:
        for c in (B_, A_):
            tile_down(c)
        for c in (A_, B_):
            for i in range(G):
                masks(c, i)
        stored = [0, 0]
        for c in (A_, B_):
            g.vector.wait_ge(sem["fm%d" % c], 2)
            for i in range(G):
                at = H * (G * c + i)
                g.vector.wait_ge(sem["u%d_%d" % (i, c)], 1)
                g.vector.tensor_tensor(T.yt[:, at:at + H], ubank(c, i), mask_at(c, 2 * i), A.mult).then_inc(sem["y%d_%d" % (i, c)], 1)
                pieces = []
                for m in range(MB):
                    lo, hi = max(H * c, NC * m), min(H * c + H, NC * m + NC)
                    if lo < hi:
                        pieces.append((lo - hi, at + lo - H * c, NC * (G * m + i) + lo - NC * m, hi - lo))
                pieces.sort()
                for j, (_, fr, to, w) in enumerate(pieces):
                    k = (i + j) % 2
                    q, st = (g.sync, g.scalar)[k], (sem.st0, sem.st1)[k]
                    q.wait_ge(sem["y%d_%d" % (i, c)], 1)
                    q.dma_start(T.y[:, to:to + w], T.yt[:, fr:fr + w]).then_inc(st, 16)
                    stored[k] += 16
        g.sync.wait_ge(sem.st0, stored[0])
        g.scalar.wait_ge(sem.st1, stored[1])
        return
    tile_down(0)
    if turn:
        masks(0, 0)
        for i in range(G):
            g.vector.wait_ge(sem["z%d_1" % i], 1)
            masks(1, i)
        tile_back(1)
        masks(0, 1)
        tile_back(0)
    else:
        tile_down(1)
        for c in (1, 0):
            for i in range(G):
                masks(c, i)
        tile_back(1)
        tile_back(0)
